import numpy as np
CORES = [56,64,184,192,312,320,440,448]
N = 8
TK = 128
D = 128 * N
EPS = 0.01
def setup_inputs(rng):
    return {"x": (rng.standard_normal((N, 128, TK), dtype=np.float32) * (0.5 + np.abs(rng.standard_normal((1, 1, TK), dtype=np.float32))) + rng.standard_normal((1, 1, TK), dtype=np.float32)), "w": (rng.standard_normal((N, 128, 128), dtype=np.float32) / 11)}
def setup_inputs_big(rng):
    d = setup_inputs(rng)
    for k in ("x", "w"): d[k] = (d[k].astype(np.float32) * 1048576.0).astype(d[k].dtype)
    return d
def setup_inputs_small(rng):
    d = setup_inputs(rng)
    for k in ("x", "w"): d[k] = (d[k].astype(np.float32) * (1 / 1048576.0)).astype(d[k].dtype)
    return d
def setup_inputs_apart(rng):
    d = setup_inputs(rng)
    f = (10.0 ** rng.permutation(np.linspace(-1.5, 1.5, N))).astype(np.float32).reshape(N, 1, 1)
    for k in ("x", "w"): d[k] = (d[k].astype(np.float32) * f).astype(d[k].dtype)
    return d
def setup_inputs_mixed(rng):
    d = setup_inputs(rng)
    f = (10.0 ** rng.uniform(-3, 3, (1, 1, TK))).astype(np.float32); shape = rng.integers(3, size=(1, 1, TK))
    for k in ("x",):
        x = d[k].astype(np.float32)
        m = x.mean(axis=(0, 1), keepdims=True); level = m + np.sign(x - m) * np.abs(x - m).mean(axis=(0, 1), keepdims=True) * rng.uniform(0.9, 1.1, x.shape).astype(np.float32)
        other = x * np.where(rng.random(x.shape) < 0.5, 0.1, 1.0).astype(np.float32)
        d[k] = (np.where(shape == 1, level, np.where(shape == 2, other, x)) * f).astype(d[k].dtype)
    return d
def reference(x, w):
    X = x.astype(np.float64)
    Z = X
    Z = Z / np.sqrt((Z ** 2).sum(axis=(0, 1)) / D + EPS)
    s = sum(w[r].astype(np.float64).T @ Z[r] for r in range(N)).astype(np.float32)
    return {"y": np.broadcast_to(s, (N,) + s.shape)}

@@ -1,0 +1,182 @@
+from concourse.bass import DstId, RemoteDMATransfer
+from concourse.mybir import AluOpType, ActivationFunctionType
+
+N = 8
+TK = 128
+D = 128 * N
+EPS = 0.01
+W = TK + 1
+WORLD = 512
+
+SCRATCH = {
+    "xs": ("sbuf", [128, TK], "float32"),
+    "ws": ("sbuf", [128, 128], "float32"),
+    "x2": ("sbuf", [128, TK], "float32"),
+    "ones": ("sbuf", [128, 128], "float32"),
+    "idd": ("sbuf", [128, 128], "float32"),
+    "own": ("sbuf", [128, W], "float32"),
+    "l0": ("sbuf", [128, W], "float32"),
+    "l1": ("sbuf", [128, W], "float32"),
+    "l2": ("sbuf", [128, W], "float32"),
+    "l3": ("sbuf", [128, W], "float32"),
+    "acc": ("sbuf", [128, W], "float32"),
+    "uq": ("sbuf", [128, 4], "float32"),
+    "dg": ("sbuf", [128, 128], "float32"),
+    "ys": ("sbuf", [128, TK], "float32"),
+    "pp": ("psum", [128, 512], "float32"),
+    "pq": ("psum", [128, 512], "float32"),
+    "pb": ("psum", [128, 512], "float32"),
+}
+SEMAPHORES = ["sx", "sw", "sc", "si", "s2", "sp", "sq", "so", "a0", "a1", "a2", "a3", "lo", "vs", "su", "sd", "sb",
+              "sy", "st"]
+
+_CACHE = {}
+
+
+def _bits(mask):
+    return [b for b in range(16) if (mask >> b) & 1]
+
+
+def _mask_of(bits):
+    m = 0
+    for b in bits:
+        m |= 1 << b
+    return m
+
+
+def _plan(T, topo):
+    if "plan" in _CACHE:
+        return _CACHE["plan"]
+    ranks = [int(c) for c in T.cores]
+    plan = {"rank": {}, "helper": {}}
+    for r in ranks:
+        near = [s for s in ranks if topo.same_plane(r, s)][0]
+        far = [s for s in ranks if topo.chip(s) == topo.chip(r) and topo.may_write(r, s)
+               and topo.rack(topo.host(s)) != topo.rack(topo.host(r))][0]
+        cross_here = [s for s in ranks if s != r and topo.host(s) == topo.host(r)][0]
+        cross_far = [s for s in ranks if s != far and topo.host(s) == topo.host(far)][0]
+        helper = [c for c in range(WORLD)
+                  if c != r and topo.host(c) == topo.host(r) and topo.chip(c) == topo.chip(r)
+                  and topo.die(c) == topo.die(r) and topo.may_write(c, cross_here) and topo.may_write(c, cross_far)][0]
+        plan["rank"][r] = {"near": near, "far": far, "helper": helper}
+        plan["helper"][helper] = {"here": cross_here, "far": cross_far}
+    _CACHE["plan"] = plan
+    return plan
+
+
+def _dst(topo, dst, src):
+    rid, pid = topo.addr(dst, src)
+    return DstId(rid=rid, pnc=pid)
+
+
+def _helper_program(g, core, T, topo, job):
+    S = T.sem
+    here, far = job["here"], job["far"]
+    bits = _bits(topo.mask(core, here) & topo.mask(core, far))
+    half = len(bits) // 2
+    m_far, m_here = _mask_of(bits[:half]), _mask_of(bits[half:])
+    g.wait_ge(S.a0, T_FEED[0])
+    g.remote_dma_fused([
+        RemoteDMATransfer(dst_ids=[_dst(topo, far, core)], dma_engine_mask=m_far, remote_sem=S.a3,
+                          srcs=[T.l0[:], T.l1[:]], dsts=[T.l3[:]], alu_op=1),
+        RemoteDMATransfer(dst_ids=[_dst(topo, here, core)], dma_engine_mask=m_here, remote_sem=S.a2,
+                          srcs=[T.l0[:], T.l1[:]], dsts=[T.l2[:]], alu_op=1),
+    ], local_sem=S.lo)
+    g.wait_ge(S.lo, len(bits))
+
+
+T_FEED = [0]
+
+
+def _feed_masks(topo, r, info, plan):
+    off = topo.mask(r, plan["rank"][info["near"]]["helper"]) & topo.mask(r, info["near"]) & topo.mask(r, info["far"])
+    on = topo.mask(r, info["helper"]) & ~off
+    return off, on
+
+
+def rank_program(g, core, T, topo):
+    plan = _plan(T, topo)
+    r0 = int(T.cores[0])
+    off0, on0 = _feed_masks(topo, r0, plan["rank"][r0], plan)
+    T_FEED[0] = len(_bits(off0)) + len(_bits(on0))
+    if core in plan["helper"]:
+        _helper_program(g, core, T, topo, plan["helper"][core])
+        return
+    if core not in plan["rank"]:
+        return
+    info = plan["rank"][core]
+    near, far, helper = info["near"], info["far"], info["helper"]
+    near_helper = plan["rank"][near]["helper"]
+    off, on = _feed_masks(topo, core, info, plan)
+    n_off, n_on = len(_bits(off)), len(_bits(on))
+    n_half = len(_bits(topo.mask(helper, near))) // 2
+    S = T.sem
+    V, A, PE, SY = g.vector, g.scalar, g.tensor, g.sync
+    add, mult = AluOpType.add, AluOpType.mult
+
+    SY.dma_start(T.xs[:], T.x[:]).then_inc(S.sx, 16)
+    A.dma_start(T.ws[:], T.w[:]).then_inc(S.sw, 16)
+    V.memset(T.idd[:], float(D)).then_inc(S.sc, 1)
+    V.memset(T.ones[:], 1.0).then_inc(S.sc, 1)
+    g.wait_ge(S.sc, 2)
+    g.affine_select(T.idd[:], T.idd[:], [[-1, 128]], AluOpType.is_equal, 0.0, 0, 1).then_inc(S.si, 1)
+
+    A.wait_ge(S.sx, 16)
+    A.activation(out=T.x2[:], in_=T.xs[:], func=ActivationFunctionType.Square).then_inc(S.s2, 1)
+    PE.wait_ge(S.sx, 16)
+    PE.wait_ge(S.sw, 16)
+    PE.matmul(T.pp[:, 0:TK], T.ws[:], T.xs[:], True, True).then_inc(S.sp, 1)
+    PE.wait_ge(S.s2, 1)
+    PE.wait_ge(S.sc, 2)
+    PE.matmul(T.pq[:, 0:1], T.x2[:], T.ones[:, 0:1], True, True).then_inc(S.sq, 1)
+    V.wait_ge(S.sp, 1)
+    V.tensor_copy(T.own[:, 0:TK], T.pp[:, 0:TK]).then_inc(S.so, 1)
+    V.wait_ge(S.sq, 1)
+    V.tensor_scalar(T.own[:, TK:W], T.pq[:, 0:1], float(D * EPS / N), None, add).then_inc(S.so, 1)
+
+    g.wait_ge(S.so, 2)
+    g.remote_dma_fused([
+        RemoteDMATransfer(dst_ids=[_dst(topo, near_helper, core)], dma_engine_mask=off, remote_sem=S.a0,
+                          src=T.own[:], dst=T.l1[:]),
+        RemoteDMATransfer(dst_ids=[_dst(topo, helper, core)], dma_engine_mask=on, remote_sem=S.a0,
+                          src=T.own[:], dst=T.l0[:]),
+    ], local_sem=S.lo)
+    rid, pid = topo.addr(near, core)
+    g.remote_dma(T.l0[:], T.own[:], S.a0, S.lo, pid, rid, off)
+
+    g.wait_ge(S.a0, n_off)
+    g.remote_dma_fused([
+        RemoteDMATransfer(dst_ids=[_dst(topo, far, core)], dma_engine_mask=off, remote_sem=S.a1,
+                          srcs=[T.own[:], T.l0[:]], dsts=[T.l1[:]], alu_op=1),
+    ], local_sem=S.lo)
+
+    V.wait_ge(S.so, 2)
+    V.wait_ge(S.a0, n_off)
+    V.tensor_tensor(T.acc[:], T.own[:], T.l0[:], add).then_inc(S.vs, 1)
+    V.wait_ge(S.a1, n_off)
+    V.wait_ge(S.vs, 1)
+    V.tensor_tensor(T.acc[:], T.acc[:], T.l1[:], add).then_inc(S.vs, 1)
+    V.wait_ge(S.a2, n_half)
+    V.wait_ge(S.a3, n_half)
+    V.tensor_tensor(T.uq[:, 0:1], T.l2[:, TK:W], T.l3[:, TK:W], add).then_inc(S.vs, 1)
+    V.wait_ge(S.vs, 3)
+    V.tensor_tensor(T.uq[:, 1:2], T.uq[:, 0:1], T.acc[:, TK:W], add).then_inc(S.vs, 1)
+    V.wait_ge(S.vs, 4)
+    V.reciprocal(T.uq[:, 2:3], T.uq[:, 1:2]).then_inc(S.su, 1)
+    V.tensor_tensor(T.acc[:, 0:TK], T.acc[:, 0:TK], T.l2[:, 0:TK], add).then_inc(S.vs, 1)
+    V.wait_ge(S.vs, 5)
+    V.tensor_tensor(T.acc[:, 0:TK], T.acc[:, 0:TK], T.l3[:, 0:TK], add).then_inc(S.vs, 1)
+
+    A.wait_ge(S.si, 1)
+    A.wait_ge(S.su, 1)
+    A.activation(out=T.dg[:], in_=T.idd[:], func=ActivationFunctionType.Sqrt, scale=T.uq[:, 2:3]).then_inc(S.sd, 1)
+    PE.wait_ge(S.sd, 1)
+    PE.matmul(T.pb[:, 0:TK], T.ones[:], T.dg[:], True, True).then_inc(S.sb, 1)
+
+    V.wait_ge(S.vs, 6)
+    V.wait_ge(S.sb, 1)
+    V.tensor_tensor(T.ys[:], T.acc[:, 0:TK], T.pb[:, 0:TK], mult).then_inc(S.sy, 1)
+    SY.wait_ge(S.sy, 1)
+    SY.dma_start(T.y[:], T.ys[:]).then_inc(S.st, 16)
+    SY.wait_ge(S.st, 16)
+    g.wait_ge(S.lo, n_off + n_on + n_off + n_off)

@@ -1,11 +1,10 @@
 from concourse.bass import DstId, RemoteDMATransfer
-from concourse.mybir import AluOpType, ActivationFunctionType
+from concourse.mybir import AluOpType, ActivationFunctionType, AxisListType
 
 N = 8
 TK = 128
 D = 128 * N
 EPS = 0.01
-W = TK + 1
 WORLD = 512
 
 SCRATCH = {
@@ -14,12 +13,14 @@ SCRATCH = {
     "x2": ("sbuf", [128, TK], "float32"),
     "ones": ("sbuf", [128, 128], "float32"),
     "idd": ("sbuf", [128, 128], "float32"),
-    "own": ("sbuf", [128, W], "float32"),
-    "l0": ("sbuf", [128, W], "float32"),
-    "l1": ("sbuf", [128, W], "float32"),
-    "l2": ("sbuf", [128, W], "float32"),
-    "l3": ("sbuf", [128, W], "float32"),
-    "acc": ("sbuf", [128, W], "float32"),
+    "own": ("sbuf", [128, TK], "float32"),
+    "qo": ("sbuf", [128, 4], "float32"),
+    "ql": ("sbuf", [128, 4], "float32"),
+    "l0": ("sbuf", [128, TK], "float32"),
+    "l1": ("sbuf", [128, TK], "float32"),
+    "l2": ("sbuf", [128, TK], "float32"),
+    "l3": ("sbuf", [128, TK], "float32"),
+    "acc": ("sbuf", [128, TK], "float32"),
     "uq": ("sbuf", [128, 4], "float32"),
     "dg": ("sbuf", [128, 128], "float32"),
     "ys": ("sbuf", [128, TK], "float32"),
@@ -27,8 +28,8 @@ SCRATCH = {
     "pq": ("psum", [128, 512], "float32"),
     "pb": ("psum", [128, 512], "float32"),
 }
-SEMAPHORES = ["sx", "sw", "sc", "si", "s2", "sp", "sq", "so", "a0", "a1", "a2", "a3", "lo", "vs", "su", "sd", "sb",
-              "sy", "st"]
+SEMAPHORES = ["sx", "sw", "sc", "si", "s2", "sp", "sq", "so", "sr", "a0", "a1", "a2", "a3", "b0", "b1", "lo", "vs",
+              "su", "sd", "sb", "sy", "st"]
 
 _CACHE = {}
 
@@ -59,7 +60,7 @@ def _plan(T, topo):
                   if c != r and topo.host(c) == topo.host(r) and topo.chip(c) == topo.chip(r)
                   and topo.die(c) == topo.die(r) and topo.may_write(c, cross_here) and topo.may_write(c, cross_far)][0]
         plan["rank"][r] = {"near": near, "far": far, "helper": helper}
-        plan["helper"][helper] = {"here": cross_here, "far": cross_far}
+        plan["helper"][helper] = {"here": cross_here, "far": cross_far, "rank": r}
     _CACHE["plan"] = plan
     return plan
 
@@ -69,114 +70,133 @@ def _dst(topo, dst, src):
     return DstId(rid=rid, pnc=pid)
 
 
-def _helper_program(g, core, T, topo, job):
-    S = T.sem
-    here, far = job["here"], job["far"]
-    bits = _bits(topo.mask(core, here) & topo.mask(core, far))
-    half = len(bits) // 2
-    m_far, m_here = _mask_of(bits[:half]), _mask_of(bits[half:])
-    g.wait_ge(S.a0, T_FEED[0])
-    g.remote_dma_fused([
-        RemoteDMATransfer(dst_ids=[_dst(topo, far, core)], dma_engine_mask=m_far, remote_sem=S.a3,
-                          srcs=[T.l0[:], T.l1[:]], dsts=[T.l3[:]], alu_op=1),
-        RemoteDMATransfer(dst_ids=[_dst(topo, here, core)], dma_engine_mask=m_here, remote_sem=S.a2,
-                          srcs=[T.l0[:], T.l1[:]], dsts=[T.l2[:]], alu_op=1),
-    ], local_sem=S.lo)
-    g.wait_ge(S.lo, len(bits))
-
-
-T_FEED = [0]
-
-
-def _feed_masks(topo, r, info, plan):
+def _feed_masks(topo, r, plan):
+    info = plan["rank"][r]
     off = topo.mask(r, plan["rank"][info["near"]]["helper"]) & topo.mask(r, info["near"]) & topo.mask(r, info["far"])
     on = topo.mask(r, info["helper"]) & ~off
     return off, on
 
 
+def _helper_program(g, core, T, topo, plan):
+    S = T.sem
+    job = plan["helper"][core]
+    here, far = job["here"], job["far"]
+    off, on = _feed_masks(topo, job["rank"], plan)
+    fed = len(_bits(off)) + len(_bits(on))
+    bits = _bits(topo.mask(core, here) & topo.mask(core, far))
+    half = len(bits) // 2
+    m_far, m_here = _mask_of(bits[:half]), _mask_of(bits[half:])
+    d_far, d_here = _dst(topo, far, core), _dst(topo, here, core)
+    g.wait_ge(S.b0, fed)
+    g.remote_dma_fused([
+        RemoteDMATransfer(dst_ids=[d_far], dma_engine_mask=m_far, remote_sem=S.b1,
+                          srcs=[T.ql[:, 0:1], T.ql[:, 1:2]], dsts=[T.ql[:, 3:4]], alu_op=1),
+        RemoteDMATransfer(dst_ids=[d_here], dma_engine_mask=m_here, remote_sem=S.b1,
+                          srcs=[T.ql[:, 0:1], T.ql[:, 1:2]], dsts=[T.ql[:, 2:3]], alu_op=1),
+    ], local_sem=S.lo)
+    g.wait_ge(S.a0, fed)
+    g.remote_dma_fused([
+        RemoteDMATransfer(dst_ids=[d_far], dma_engine_mask=m_far, remote_sem=S.a3,
+                          srcs=[T.l0[:], T.l1[:]], dsts=[T.l3[:]], alu_op=1),
+        RemoteDMATransfer(dst_ids=[d_here], dma_engine_mask=m_here, remote_sem=S.a2,
+                          srcs=[T.l0[:], T.l1[:]], dsts=[T.l2[:]], alu_op=1),
+    ], local_sem=S.lo)
+    g.wait_ge(S.lo, 2 * len(bits))
+
+
 def rank_program(g, core, T, topo):
     plan = _plan(T, topo)
-    r0 = int(T.cores[0])
-    off0, on0 = _feed_masks(topo, r0, plan["rank"][r0], plan)
-    T_FEED[0] = len(_bits(off0)) + len(_bits(on0))
     if core in plan["helper"]:
-        _helper_program(g, core, T, topo, plan["helper"][core])
+        _helper_program(g, core, T, topo, plan)
         return
     if core not in plan["rank"]:
         return
     info = plan["rank"][core]
     near, far, helper = info["near"], info["far"], info["helper"]
     near_helper = plan["rank"][near]["helper"]
-    off, on = _feed_masks(topo, core, info, plan)
+    off, on = _feed_masks(topo, core, plan)
     n_off, n_on = len(_bits(off)), len(_bits(on))
     n_half = len(_bits(topo.mask(helper, near))) // 2
+    d_nh, d_h, d_far = _dst(topo, near_helper, core), _dst(topo, helper, core), _dst(topo, far, core)
+    rid_n, pid_n = topo.addr(near, core)
     S = T.sem
     V, A, PE, SY = g.vector, g.scalar, g.tensor, g.sync
     add, mult = AluOpType.add, AluOpType.mult
 
     SY.dma_start(T.xs[:], T.x[:]).then_inc(S.sx, 16)
     A.dma_start(T.ws[:], T.w[:]).then_inc(S.sw, 16)
-    V.memset(T.idd[:], float(D)).then_inc(S.sc, 1)
     V.memset(T.ones[:], 1.0).then_inc(S.sc, 1)
+    V.memset(T.idd[:], float(D)).then_inc(S.sc, 1)
     g.wait_ge(S.sc, 2)
     g.affine_select(T.idd[:], T.idd[:], [[-1, 128]], AluOpType.is_equal, 0.0, 0, 1).then_inc(S.si, 1)
 
     A.wait_ge(S.sx, 16)
     A.activation(out=T.x2[:], in_=T.xs[:], func=ActivationFunctionType.Square).then_inc(S.s2, 1)
+    PE.wait_ge(S.sc, 2)
+    PE.wait_ge(S.s2, 1)
+    PE.matmul(T.pq[:, 0:1], T.x2[:], T.ones[:, 0:1], True, True).then_inc(S.sq, 1)
     PE.wait_ge(S.sx, 16)
     PE.wait_ge(S.sw, 16)
     PE.matmul(T.pp[:, 0:TK], T.ws[:], T.xs[:], True, True).then_inc(S.sp, 1)
-    PE.wait_ge(S.s2, 1)
-    PE.wait_ge(S.sc, 2)
-    PE.matmul(T.pq[:, 0:1], T.x2[:], T.ones[:, 0:1], True, True).then_inc(S.sq, 1)
-    V.wait_ge(S.sp, 1)
-    V.tensor_copy(T.own[:, 0:TK], T.pp[:, 0:TK]).then_inc(S.so, 1)
     V.wait_ge(S.sq, 1)
-    V.tensor_scalar(T.own[:, TK:W], T.pq[:, 0:1], float(D * EPS / N), None, add).then_inc(S.so, 1)
+    V.tensor_scalar(T.qo[:, 0:1], T.pq[:, 0:1], float(D * EPS / N), None, add).then_inc(S.sr, 1)
+    V.wait_ge(S.sp, 1)
+    V.tensor_copy(T.own[:], T.pp[:, 0:TK]).then_inc(S.so, 1)
 
-    g.wait_ge(S.so, 2)
+    g.wait_ge(S.sr, 1)
     g.remote_dma_fused([
-        RemoteDMATransfer(dst_ids=[_dst(topo, near_helper, core)], dma_engine_mask=off, remote_sem=S.a0,
-                          src=T.own[:], dst=T.l1[:]),
-        RemoteDMATransfer(dst_ids=[_dst(topo, helper, core)], dma_engine_mask=on, remote_sem=S.a0,
-                          src=T.own[:], dst=T.l0[:]),
+        RemoteDMATransfer(dst_ids=[d_nh], dma_engine_mask=off, remote_sem=S.b0, src=T.qo[:, 0:1], dst=T.ql[:, 1:2]),
+        RemoteDMATransfer(dst_ids=[d_h], dma_engine_mask=on, remote_sem=S.b0, src=T.qo[:, 0:1], dst=T.ql[:, 0:1]),
     ], local_sem=S.lo)
-    rid, pid = topo.addr(near, core)
-    g.remote_dma(T.l0[:], T.own[:], S.a0, S.lo, pid, rid, off)
+    g.remote_dma(T.ql[:, 0:1], T.qo[:, 0:1], S.b0, S.lo, pid_n, rid_n, off)
+    g.wait_ge(S.so, 1)
+    g.remote_dma_fused([
+        RemoteDMATransfer(dst_ids=[d_nh], dma_engine_mask=off, remote_sem=S.a0, src=T.own[:], dst=T.l1[:]),
+        RemoteDMATransfer(dst_ids=[d_h], dma_engine_mask=on, remote_sem=S.a0, src=T.own[:], dst=T.l0[:]),
+    ], local_sem=S.lo)
+    g.remote_dma(T.l0[:], T.own[:], S.a0, S.lo, pid_n, rid_n, off)
 
+    g.wait_ge(S.b0, n_off)
+    g.remote_dma_fused([
+        RemoteDMATransfer(dst_ids=[d_far], dma_engine_mask=off, remote_sem=S.b1,
+                          srcs=[T.qo[:, 0:1], T.ql[:, 0:1]], dsts=[T.ql[:, 1:2]], alu_op=1),
+    ], local_sem=S.lo)
     g.wait_ge(S.a0, n_off)
     g.remote_dma_fused([
-        RemoteDMATransfer(dst_ids=[_dst(topo, far, core)], dma_engine_mask=off, remote_sem=S.a1,
+        RemoteDMATransfer(dst_ids=[d_far], dma_engine_mask=off, remote_sem=S.a1,
                           srcs=[T.own[:], T.l0[:]], dsts=[T.l1[:]], alu_op=1),
     ], local_sem=S.lo)
 
-    V.wait_ge(S.so, 2)
+    V.wait_ge(S.so, 1)
     V.wait_ge(S.a0, n_off)
-    V.tensor_tensor(T.acc[:], T.own[:], T.l0[:], add).then_inc(S.vs, 1)
-    V.wait_ge(S.a1, n_off)
-    V.wait_ge(S.vs, 1)
-    V.tensor_tensor(T.acc[:], T.acc[:], T.l1[:], add).then_inc(S.vs, 1)
-    V.wait_ge(S.a2, n_half)
-    V.wait_ge(S.a3, n_half)
-    V.tensor_tensor(T.uq[:, 0:1], T.l2[:, TK:W], T.l3[:, TK:W], add).then_inc(S.vs, 1)
-    V.wait_ge(S.vs, 3)
-    V.tensor_tensor(T.uq[:, 1:2], T.uq[:, 0:1], T.acc[:, TK:W], add).then_inc(S.vs, 1)
-    V.wait_ge(S.vs, 4)
-    V.reciprocal(T.uq[:, 2:3], T.uq[:, 1:2]).then_inc(S.su, 1)
-    V.tensor_tensor(T.acc[:, 0:TK], T.acc[:, 0:TK], T.l2[:, 0:TK], add).then_inc(S.vs, 1)
-    V.wait_ge(S.vs, 5)
-    V.tensor_tensor(T.acc[:, 0:TK], T.acc[:, 0:TK], T.l3[:, 0:TK], add).then_inc(S.vs, 1)
+    V.tensor_tensor(T.pp[:, 0:TK], T.pp[:, 0:TK], T.l0[:], add).then_inc(S.vs, 1)
 
+    V.wait_ge(S.b0, n_off)
+    V.wait_ge(S.b1, n_off + 2 * n_half)
+    V.tensor_reduce(T.uq[:, 0:1], T.ql[:, 0:4], AxisListType.X, add).then_inc(S.vs, 1)
+    V.wait_ge(S.sr, 1)
+    V.wait_ge(S.vs, 2)
+    V.tensor_tensor(T.uq[:, 1:2], T.uq[:, 0:1], T.qo[:, 0:1], add).then_inc(S.vs, 1)
+    V.wait_ge(S.vs, 3)
+    V.reciprocal(T.uq[:, 2:3], T.uq[:, 1:2]).then_inc(S.su, 1)
     A.wait_ge(S.si, 1)
     A.wait_ge(S.su, 1)
     A.activation(out=T.dg[:], in_=T.idd[:], func=ActivationFunctionType.Sqrt, scale=T.uq[:, 2:3]).then_inc(S.sd, 1)
     PE.wait_ge(S.sd, 1)
     PE.matmul(T.pb[:, 0:TK], T.ones[:], T.dg[:], True, True).then_inc(S.sb, 1)
 
+    V.wait_ge(S.a1, n_off)
+    V.tensor_tensor(T.pp[:, 0:TK], T.pp[:, 0:TK], T.l1[:], add).then_inc(S.vs, 1)
+    V.wait_ge(S.a2, n_half)
+    V.wait_ge(S.vs, 4)
+    V.tensor_tensor(T.pp[:, 0:TK], T.pp[:, 0:TK], T.l2[:], add).then_inc(S.vs, 1)
+    V.wait_ge(S.a3, n_half)
+    V.wait_ge(S.vs, 5)
+    V.tensor_tensor(T.acc[:], T.pp[:, 0:TK], T.l3[:], add).then_inc(S.vs, 1)
     V.wait_ge(S.vs, 6)
     V.wait_ge(S.sb, 1)
-    V.tensor_tensor(T.ys[:], T.acc[:, 0:TK], T.pb[:, 0:TK], mult).then_inc(S.sy, 1)
+    V.tensor_tensor(T.ys[:], T.acc[:], T.pb[:, 0:TK], mult).then_inc(S.sy, 1)
     SY.wait_ge(S.sy, 1)
     SY.dma_start(T.y[:], T.ys[:]).then_inc(S.st, 16)
     SY.wait_ge(S.st, 16)
-    g.wait_ge(S.lo, n_off + n_on + n_off + n_off)
+    g.wait_ge(S.lo, 6 * n_off + 2 * n_on)

from concourse.bass import DstId, RemoteDMATransfer
from concourse.mybir import AluOpType, ActivationFunctionType, AxisListType

N = 8
TK = 128
D = 128 * N
EPS = 0.01
WORLD = 512

SCRATCH = {
    "xs": ("sbuf", [128, TK], "float32"),
    "ws": ("sbuf", [128, 128], "float32"),
    "x2": ("sbuf", [128, TK], "float32"),
    "ones": ("sbuf", [128, 128], "float32"),
    "idd": ("sbuf", [128, 128], "float32"),
    "own": ("sbuf", [128, TK], "float32"),
    "qo": ("sbuf", [128, 4], "float32"),
    "ql": ("sbuf", [128, 4], "float32"),
    "l0": ("sbuf", [128, TK], "float32"),
    "l1": ("sbuf", [128, TK], "float32"),
    "l2": ("sbuf", [128, TK], "float32"),
    "l3": ("sbuf", [128, TK], "float32"),
    "acc": ("sbuf", [128, TK], "float32"),
    "uq": ("sbuf", [128, 4], "float32"),
    "dg": ("sbuf", [128, 128], "float32"),
    "ys": ("sbuf", [128, TK], "float32"),
    "pp": ("psum", [128, 512], "float32"),
    "pq": ("psum", [128, 512], "float32"),
    "pb": ("psum", [128, 512], "float32"),
}
SEMAPHORES = ["sx", "sw", "sc", "si", "s2", "sp", "sq", "so", "sr", "a0", "a1", "a2", "a3", "b0", "b1", "lo", "vs",
              "su", "sd", "sb", "sy", "st"]

_CACHE = {}


def _bits(mask):
    return [b for b in range(16) if (mask >> b) & 1]


def _mask_of(bits):
    m = 0
    for b in bits:
        m |= 1 << b
    return m


def _plan(T, topo):
    if "plan" in _CACHE:
        return _CACHE["plan"]
    ranks = [int(c) for c in T.cores]
    plan = {"rank": {}, "helper": {}}
    for r in ranks:
        near = [s for s in ranks if topo.same_plane(r, s)][0]
        far = [s for s in ranks if topo.chip(s) == topo.chip(r) and topo.may_write(r, s)
               and topo.rack(topo.host(s)) != topo.rack(topo.host(r))][0]
        cross_here = [s for s in ranks if s != r and topo.host(s) == topo.host(r)][0]
        cross_far = [s for s in ranks if s != far and topo.host(s) == topo.host(far)][0]
        helper = [c for c in range(WORLD)
                  if c != r and topo.host(c) == topo.host(r) and topo.chip(c) == topo.chip(r)
                  and topo.die(c) == topo.die(r) and topo.may_write(c, cross_here) and topo.may_write(c, cross_far)][0]
        plan["rank"][r] = {"near": near, "far": far, "helper": helper}
        plan["helper"][helper] = {"here": cross_here, "far": cross_far, "rank": r}
    _CACHE["plan"] = plan
    return plan


def _dst(topo, dst, src):
    rid, pid = topo.addr(dst, src)
    return DstId(rid=rid, pnc=pid)


def _feed_masks(topo, r, plan):
    info = plan["rank"][r]
    off = topo.mask(r, plan["rank"][info["near"]]["helper"]) & topo.mask(r, info["near"]) & topo.mask(r, info["far"])
    on = topo.mask(r, info["helper"]) & ~off
    return off, on


def _helper_program(g, core, T, topo, plan):
    S = T.sem
    job = plan["helper"][core]
    here, far = job["here"], job["far"]
    off, on = _feed_masks(topo, job["rank"], plan)
    fed = len(_bits(off)) + len(_bits(on))
    bits = _bits(topo.mask(core, here) & topo.mask(core, far))
    half = len(bits) // 2
    m_far, m_here = _mask_of(bits[:half]), _mask_of(bits[half:])
    d_far, d_here = _dst(topo, far, core), _dst(topo, here, core)
    g.wait_ge(S.b0, fed)
    g.remote_dma_fused([
        RemoteDMATransfer(dst_ids=[d_far], dma_engine_mask=m_far, remote_sem=S.b1,
                          srcs=[T.ql[:, 0:1], T.ql[:, 1:2]], dsts=[T.ql[:, 3:4]], alu_op=1),
        RemoteDMATransfer(dst_ids=[d_here], dma_engine_mask=m_here, remote_sem=S.b1,
                          srcs=[T.ql[:, 0:1], T.ql[:, 1:2]], dsts=[T.ql[:, 2:3]], alu_op=1),
    ], local_sem=S.lo)
    g.wait_ge(S.a0, fed)
    g.remote_dma_fused([
        RemoteDMATransfer(dst_ids=[d_far], dma_engine_mask=m_far, remote_sem=S.a3,
                          srcs=[T.l0[:], T.l1[:]], dsts=[T.l3[:]], alu_op=1),
        RemoteDMATransfer(dst_ids=[d_here], dma_engine_mask=m_here, remote_sem=S.a2,
                          srcs=[T.l0[:], T.l1[:]], dsts=[T.l2[:]], alu_op=1),
    ], local_sem=S.lo)
    g.wait_ge(S.lo, 2 * len(bits))


def rank_program(g, core, T, topo):
    plan = _plan(T, topo)
    if core in plan["helper"]:
        _helper_program(g, core, T, topo, plan)
        return
    if core not in plan["rank"]:
        return
    info = plan["rank"][core]
    near, far, helper = info["near"], info["far"], info["helper"]
    near_helper = plan["rank"][near]["helper"]
    off, on = _feed_masks(topo, core, plan)
    n_off, n_on = len(_bits(off)), len(_bits(on))
    n_half = len(_bits(topo.mask(helper, near))) // 2
    d_nh, d_h, d_far = _dst(topo, near_helper, core), _dst(topo, helper, core), _dst(topo, far, core)
    rid_n, pid_n = topo.addr(near, core)
    S = T.sem
    V, A, PE, SY = g.vector, g.scalar, g.tensor, g.sync
    add, mult = AluOpType.add, AluOpType.mult

    SY.dma_start(T.xs[:], T.x[:]).then_inc(S.sx, 16)
    A.dma_start(T.ws[:], T.w[:]).then_inc(S.sw, 16)
    V.memset(T.ones[:], 1.0).then_inc(S.sc, 1)
    V.memset(T.idd[:], float(D)).then_inc(S.sc, 1)
    g.wait_ge(S.sc, 2)
    g.affine_select(T.idd[:], T.idd[:], [[-1, 128]], AluOpType.is_equal, 0.0, 0, 1).then_inc(S.si, 1)

    A.wait_ge(S.sx, 16)
    A.activation(out=T.x2[:], in_=T.xs[:], func=ActivationFunctionType.Square).then_inc(S.s2, 1)
    PE.wait_ge(S.sc, 2)
    PE.wait_ge(S.s2, 1)
    PE.matmul(T.pq[:, 0:1], T.x2[:], T.ones[:, 0:1], True, True).then_inc(S.sq, 1)
    PE.wait_ge(S.sx, 16)
    PE.wait_ge(S.sw, 16)
    PE.matmul(T.pp[:, 0:TK], T.ws[:], T.xs[:], True, True).then_inc(S.sp, 1)
    V.wait_ge(S.sq, 1)
    V.tensor_scalar(T.qo[:, 0:1], T.pq[:, 0:1], float(D * EPS / N), None, add).then_inc(S.sr, 1)
    V.wait_ge(S.sp, 1)
    V.tensor_copy(T.own[:], T.pp[:, 0:TK]).then_inc(S.so, 1)

    g.wait_ge(S.sr, 1)
    g.remote_dma_fused([
        RemoteDMATransfer(dst_ids=[d_nh], dma_engine_mask=off, remote_sem=S.b0, src=T.qo[:, 0:1], dst=T.ql[:, 1:2]),
        RemoteDMATransfer(dst_ids=[d_h], dma_engine_mask=on, remote_sem=S.b0, src=T.qo[:, 0:1], dst=T.ql[:, 0:1]),
    ], local_sem=S.lo)
    g.remote_dma(T.ql[:, 0:1], T.qo[:, 0:1], S.b0, S.lo, pid_n, rid_n, off)
    g.wait_ge(S.so, 1)
    g.remote_dma_fused([
        RemoteDMATransfer(dst_ids=[d_nh], dma_engine_mask=off, remote_sem=S.a0, src=T.own[:], dst=T.l1[:]),
        RemoteDMATransfer(dst_ids=[d_h], dma_engine_mask=on, remote_sem=S.a0, src=T.own[:], dst=T.l0[:]),
    ], local_sem=S.lo)
    g.remote_dma(T.l0[:], T.own[:], S.a0, S.lo, pid_n, rid_n, off)

    g.wait_ge(S.b0, n_off)
    g.remote_dma_fused([
        RemoteDMATransfer(dst_ids=[d_far], dma_engine_mask=off, remote_sem=S.b1,
                          srcs=[T.qo[:, 0:1], T.ql[:, 0:1]], dsts=[T.ql[:, 1:2]], alu_op=1),
    ], local_sem=S.lo)
    g.wait_ge(S.a0, n_off)
    g.remote_dma_fused([
        RemoteDMATransfer(dst_ids=[d_far], dma_engine_mask=off, remote_sem=S.a1,
                          srcs=[T.own[:], T.l0[:]], dsts=[T.l1[:]], alu_op=1),
    ], local_sem=S.lo)

    V.wait_ge(S.so, 1)
    V.wait_ge(S.a0, n_off)
    V.tensor_tensor(T.pp[:, 0:TK], T.pp[:, 0:TK], T.l0[:], add).then_inc(S.vs, 1)

    V.wait_ge(S.b0, n_off)
    V.wait_ge(S.b1, n_off + 2 * n_half)
    V.tensor_reduce(T.uq[:, 0:1], T.ql[:, 0:4], AxisListType.X, add).then_inc(S.vs, 1)
    V.wait_ge(S.sr, 1)
    V.wait_ge(S.vs, 2)
    V.tensor_tensor(T.uq[:, 1:2], T.uq[:, 0:1], T.qo[:, 0:1], add).then_inc(S.vs, 1)
    V.wait_ge(S.vs, 3)
    V.reciprocal(T.uq[:, 2:3], T.uq[:, 1:2]).then_inc(S.su, 1)
    A.wait_ge(S.si, 1)
    A.wait_ge(S.su, 1)
    A.activation(out=T.dg[:], in_=T.idd[:], func=ActivationFunctionType.Sqrt, scale=T.uq[:, 2:3]).then_inc(S.sd, 1)
    PE.wait_ge(S.sd, 1)
    PE.matmul(T.pb[:, 0:TK], T.ones[:], T.dg[:], True, True).then_inc(S.sb, 1)

    V.wait_ge(S.a1, n_off)
    V.tensor_tensor(T.pp[:, 0:TK], T.pp[:, 0:TK], T.l1[:], add).then_inc(S.vs, 1)
    V.wait_ge(S.a2, n_half)
    V.wait_ge(S.vs, 4)
    V.tensor_tensor(T.pp[:, 0:TK], T.pp[:, 0:TK], T.l2[:], add).then_inc(S.vs, 1)
    V.wait_ge(S.a3, n_half)
    V.wait_ge(S.vs, 5)
    V.tensor_tensor(T.acc[:], T.pp[:, 0:TK], T.l3[:], add).then_inc(S.vs, 1)
    V.wait_ge(S.vs, 6)
    V.wait_ge(S.sb, 1)
    V.tensor_tensor(T.ys[:], T.acc[:], T.pb[:, 0:TK], mult).then_inc(S.sy, 1)
    SY.wait_ge(S.sy, 1)
    SY.dma_start(T.y[:], T.ys[:]).then_inc(S.st, 16)
    SY.wait_ge(S.st, 16)
    g.wait_ge(S.lo, 6 * n_off + 2 * n_on)
